import numpy as np
import ml_dtypes


def mxq(x, axis, fmt="e4m3"):
    dtype, down = {"e4m3": (ml_dtypes.float8_e4m3fn, 7), "e5m2": (ml_dtypes.float8_e5m2, 14)}[fmt]
    v = np.moveaxis(np.asarray(x, np.float32).astype(ml_dtypes.bfloat16).astype(np.float64), axis, -1)
    blocks = v.reshape(v.shape[:-1] + (-1, 32))
    amax = np.abs(blocks).max(-1, keepdims=True)
    byte = np.maximum(np.where(amax > 0, np.frexp(amax)[1] - 1 + 127, 0) - down, 1)
    scale = np.exp2(byte - 127.0)
    codes = (blocks / scale).astype(np.float32).astype(dtype).astype(np.float64)
    return np.moveaxis((codes * scale).reshape(v.shape), -1, axis)


WIDE = False


def mx_kscale(k):
    if not WIDE:
        return np.ones(k)
    levels = np.array([10, -10, 5, -5, 0])
    if k % 512:
        return np.exp2(np.random.permutation(np.resize(levels, k // 32))).repeat(32)
    a = np.empty((k // 512, 16))
    for p in range(k // 512):
        a[p, :8] = np.random.permutation(np.resize(levels, 8))
        for g in range(8):
            far = levels[np.abs(levels - a[p, g]) >= 10]
            a[p, g + 8] = far[np.random.randint(len(far))]
    return np.exp2(a.ravel()).repeat(32)


def f64(x):
    return np.asarray(x).astype(np.float64)


def striped(idx):
    return np.tile(idx.reshape(-1, 16).T, (8, 1)).astype(np.uint16)


def unstriped(offs):
    return offs[:16].T.reshape(-1).astype(np.int64)


E2M1 = np.array([0.0, 0.5, 1.0, 1.5, 2.0, 3.0, 4.0, 6.0, -0.0, -0.5, -1.0, -1.5, -2.0, -3.0, -4.0, -6.0])


def pack_weight(w, fmt):
    k, n = w.shape
    w = f64(np.asarray(w, np.float32).astype(ml_dtypes.bfloat16)).reshape(k // 32, 32, n)
    amax = np.abs(w).max(1)
    if fmt == "e4m3":
        byte = np.frexp(amax)[1] - 1 + 127 - 7
    else:
        mant, ex = np.frexp(amax / 6.0)
        byte = np.where(mant > 0.5, ex, ex - 1) + 127
    byte = np.clip(np.where(amax > 0, byte, 1), 1, 254)
    scaled = (w * np.exp2(127.0 - byte)[:, None, :]).reshape(k, n).astype(np.float32)
    by_word = np.ascontiguousarray(scaled.reshape(k // 512, 128, 4, n).transpose(0, 1, 3, 2))
    if fmt == "e4m3":
        words = by_word.astype(ml_dtypes.float8_e4m3fn).view(np.uint8)
    else:
        c = by_word.astype(ml_dtypes.float4_e2m1fn).view(np.uint8) & 0xF
        words = (c[..., 0::2] | (c[..., 1::2] << 4)).reshape(k // 512, 128, 2 * n)
    return np.ascontiguousarray(words), np.ascontiguousarray(byte.astype(np.uint8).reshape(k // 512, 16, n))


def unpack_weight(words, scales, fmt):
    g, _, n = scales.shape
    words = np.ascontiguousarray(words).reshape(g, 128, n, -1)
    if fmt == "e4m3":
        vals = words.view(ml_dtypes.float8_e4m3fn).astype(np.float64)
    else:
        nib = np.empty((g, 128, n, 4), np.uint8)
        nib[..., 0::2] = words & 0xF
        nib[..., 1::2] = words >> 4
        vals = E2M1[nib]
    vals = vals * np.repeat(np.exp2(scales.astype(np.float64) - 127.0), 8, axis=1)[..., None]
    return vals.transpose(0, 1, 3, 2).reshape(g * 512, n)


def gelu(v):
    return 0.5 * v * (1.0 + np.tanh(np.sqrt(2.0 / np.pi) * (v + 0.044715 * v**3)))


def bf(x):
    return np.asarray(x, np.float32).astype(ml_dtypes.bfloat16)


def planes(Y):
    n, m = Y.shape
    b = f64(bf(Y)).reshape(n // 32, 32, m)
    amax = np.abs(b).max(1)
    byte = np.clip(np.where(amax > 0, np.frexp(amax)[1] - 1 + 127 - 7, 1), 1, 254)
    codes = (b * np.exp2(127.0 - byte)[:, None, :]).reshape(n, m).astype(np.float32).astype(ml_dtypes.float8_e4m3fn).view(np.uint8)
    words = codes.reshape(n // 512, 128, 4, m).transpose(0, 1, 3, 2)
    return np.ascontiguousarray(words), np.ascontiguousarray(byte.astype(np.uint8).reshape(n // 512, 16, m))


K, T, S, P, H, N = 1024, 4096, 1024, 512, 1024, 512

def setup_inputs():
    n = np.random.standard_normal
    s = mx_kscale(K)[:, None]
    u = mx_kscale(H)[:, None]
    spread = np.exp(0.8 * n(N))
    tab_words, tab_scales = pack_weight(n((K, T)) * s, "e4m3")
    w1 = n((K, H)) / np.sqrt(K) / s * u.T
    wa_words, wa_scales = pack_weight(1.1 * n((H, N)) / np.sqrt(H) / u, "e2m1")
    wb = n((H, N)) / np.sqrt(H) / u * spread[None, :]
    swing = np.sign(n(N) - 0.4) * np.random.uniform(1.5, 3.5, N) * spread
    return {
        "tab_words": tab_words, "tab_scales": tab_scales,
        "offs": striped(np.random.permutation(T)[:S]),
        "pos1": striped(np.random.permutation(S)[:P]),
        "pos2": striped(np.random.permutation(S)[:P]),
        "w1": w1.astype(np.float32),
        "leak": np.random.uniform(0.05, 0.6, H).astype(np.float32),
        "wa_words": wa_words, "wa_scales": wa_scales,
        "wb": wb.astype(np.float32),
        "site": (0.7 * n((N, S)) * spread[:, None]).astype(np.float32),
        "steep": np.random.uniform(0.6, 3.0, N).astype(np.float32),
        "thresh": n(N).astype(np.float32),
        "swing": swing.astype(np.float32),
    }

def reference(tab_words, tab_scales, offs, pos1, pos2, w1, leak, wa_words, wa_scales, wb, site, steep, thresh, swing):
    v = unpack_weight(tab_words, tab_scales, "e4m3")[:, unstriped(offs)]
    p = mxq(f64(w1), 0, "e4m3").T @ v
    h = np.maximum(p, f64(leak)[:, None] * p)
    hq = mxq(h, 0, "e4m3")
    e = unpack_weight(wa_words, wa_scales, "e2m1").T @ hq
    d = (mxq(f64(wb), 0, "e4m3").T @ hq) + f64(site)
    gate = 1.0 / (1.0 + np.exp(-(f64(steep)[:, None] * e[:, unstriped(pos1)] + f64(thresh)[:, None])))
    a = f64(swing)[:, None] * gate
    c = d[:, unstriped(pos2)]
    y = np.minimum(a, c) + c
    words, scales = planes(y)
    return y, words, scales

@@ -1,0 +1,235 @@
+from contextlib import ExitStack
+
+import concourse.mybir as mybir
+
+F32 = mybir.dt.float32
+BF16 = mybir.dt.bfloat16
+I32 = mybir.dt.int32
+U32 = mybir.dt.uint32
+U16 = mybir.dt.uint16
+U8 = mybir.dt.uint8
+FP8X4 = mybir.dt.float8_e4m3fn_x4
+FP4X4 = mybir.dt.float4_e2m1fn_x4
+ALU = mybir.AluOpType
+ACT = mybir.ActivationFunctionType
+
+K, T, S, NP, H, N = 1024, 4096, 1024, 512, 1024, 512
+FLOPS = 2 * K * H * S + 2 * 2 * H * N * S
+P = 128
+
+
+def cast(nc, eng, dst, raw, m0, m1):
+    o = dst[:].rearrange("p t m j -> p m t j")[:, m0:m1]
+    i = raw.rearrange("p j (m t) -> p m t j", t=4)
+    if eng == "v":
+        nc.vector.tensor_copy(out=o, in_=i)
+    elif eng == "s":
+        nc.scalar.copy(out=o, in_=i)
+    else:
+        nc.gpsimd.tensor_scalar(out=o, in0=i, scalar1=1.0, scalar2=0.0, op0=ALU.mult, op1=ALU.add)
+
+
+def tile_list_roaming_gate_scores_kernel(tc, tab_words, tab_scales, offs, pos1, pos2, w1, leak, wa_words, wa_scales, wb, site, steep, thresh, swing, out_0, out_1, out_2):
+    nc = tc.nc
+    with ExitStack() as ctx:
+        keep = ctx.enter_context(tc.tile_pool(name="keep", bufs=1))
+        ring = ctx.enter_context(tc.tile_pool(name="ring", bufs=3))
+        ps1 = ctx.enter_context(tc.psum_pool(name="ps1", bufs=4))
+        ps2 = ctx.enter_context(tc.psum_pool(name="ps2", bufs=4))
+
+        def kt(shape, dt, name, tag=None):
+            return keep.tile(shape, dt, name=name, tag=tag or name, align_bytes=64)
+
+        offs_t = keep.tile([P, S // 16], U16, name="offs_t")
+        pos1_t = keep.tile([P, NP // 16], U16, name="pos1_t")
+        pos2_t = keep.tile([P, NP // 16], U16, name="pos2_t")
+        tabw = [kt([P, T], I32, "tabw%d" % a) for a in range(2)]
+        tabs = kt([P, T], U8, "tabs")
+        was_raw = kt([P, 2, N], U8, "was_raw")
+        waw_raw = kt([P, 2, 2 * N], U8, "waw_raw")
+        nc.vector.memset(tabs[:].bitcast(I32), 0)
+        nc.vector.memset(was_raw[:].bitcast(I32), 0)
+
+        nc.sync.dma_start(offs_t[:], offs)
+        for a in range(2):
+            nc.sync.dma_start(out=tabw[a][:], in_=tab_words[a].rearrange("p t i -> p (t i)").bitcast(I32))
+        for q in range(4):
+            nc.gpsimd.dma_start(out=tabs[32 * q : 32 * q + 8, :].bitcast(I32), in_=tab_scales[:, 4 * q : 4 * q + 4, :].bitcast(I32))
+        leak_t = kt([P, 2, 4], F32, "leak_t")
+        nc.gpsimd.dma_start(out=leak_t[:], in_=leak.rearrange("(b p t) -> p b t", b=2, t=4))
+        for q in range(4):
+            nc.gpsimd.dma_start(out=was_raw[32 * q : 32 * q + 4].bitcast(I32), in_=wa_scales[:, 4 * q : 4 * q + 4, :].rearrange("a r c -> r a c").bitcast(I32))
+        vecs = []
+        for nm, v in (("steep_t", steep), ("thresh_t", thresh), ("swing_t", swing)):
+            vt = kt([P, 4], F32, nm)
+            nc.gpsimd.dma_start(out=vt[:], in_=v.rearrange("(p t) -> p t", t=4))
+            vecs.append(vt)
+        steep_t, thresh_t, swing_t = vecs
+        nc.sync.dma_start(out=waw_raw[:].bitcast(I32), in_=wa_words.rearrange("a p c -> p a c").bitcast(I32))
+
+        w1_raw = {}
+        for a, b, halves in ((0, 0, 1), (1, 0, 2), (0, 1, 1), (1, 1, 1)):
+            w = 512 // halves
+            for hf in range(halves):
+                r = kt([P, 4, w], F32, "w1r%d%d%d" % (a, b, hf))
+                c0 = 512 * b + w * hf
+                nc.sync.dma_start(out=r[:], in_=w1[512 * a : 512 * a + 512, c0 : c0 + w].rearrange("(p j) c -> p j c", j=4))
+                w1_raw[(a, b, hf)] = r
+        wb_raw = []
+        for b in range(2):
+            r = kt([P, 4, N], F32, "wbr%d" % b)
+            nc.sync.dma_start(out=r[:], in_=wb[512 * b : 512 * b + 512, :].rearrange("(p j) c -> p j c", j=4))
+            wb_raw.append(r)
+        nc.sync.dma_start(pos1_t[:], pos1)
+        nc.sync.dma_start(pos2_t[:], pos2)
+        site_v = site.rearrange("(p t) j -> t p j", t=4)
+        site_t = []
+        for t in range(4):
+            r = kt([P, S], F32, "site%d" % t, ("w1r000", "w1r100", "w1r101", None)[t])
+            nc.sync.dma_start(out=r[:], in_=site_v[t])
+            site_t.append(r)
+
+        vs = kt([P, S], U8, "vs")
+        nc.vector.tensor_copy(out=vs[:], in_=tabs[:].indirect(offs_t[:]))
+        vw = [kt([P, S], U32, "vw%d" % a) for a in range(2)]
+        nc.vector.tensor_copy(out=vw[0][:], in_=tabw[0][:].bitcast(U32).indirect(offs_t[:]))
+        waw = kt([P, 2, 2 * N], U8, "waw")
+        was = kt([P, 2, N], U8, "was")
+        for a in range(2):
+            nc.vector.tensor_copy(out=waw[:, a, :].rearrange("p (t m e) -> p t m e", t=4, e=2), in_=waw_raw[:, a, :].rearrange("p (m t e) -> p t m e", t=4, e=2))
+        nc.vector.tensor_copy(out=was[:].rearrange("p a (t m) -> p a t m", t=4), in_=was_raw[:].rearrange("p a (m t) -> p a t m", t=4))
+        nc.vector.tensor_copy(out=vw[1][:], in_=tabw[1][:].bitcast(U32).indirect(offs_t[:]))
+
+        def quant(src, width, name):
+            codes = kt([P, width], U32, name + "_c")
+            scales = kt([P, width], U8, name + "_s")
+            nc.vector.quantize_mx(out=codes[:].bitcast(FP8X4), scales=scales[:], in_=src)
+            return codes, scales
+
+        def weight(name, pieces):
+            g = kt([P, 4, P, 4], BF16, name + "_g")
+            for eng, raw, c0, m0, m1 in pieces:
+                cast(nc, eng, g, raw[:, :, c0 : c0 + 4 * (m1 - m0)], m0, m1)
+            return g
+
+        def wq(g, name):
+            return quant(g[:].rearrange("p t m j -> p (t m j)"), 512, name)
+
+        w1q = {}
+        r = w1_raw[(0, 0, 0)]
+        w1q[(0, 0)] = wq(weight("w00", [("s", r, 0, 0, 48), ("v", r, 192, 48, 128)]), "w00")
+        r0, r1 = w1_raw[(1, 0, 0)], w1_raw[(1, 0, 1)]
+        w1q[(1, 0)] = wq(weight("w10", [("s", r0, 0, 0, 64), ("s", r1, 0, 64, 80), ("v", r1, 64, 80, 128)]), "w10")
+        r = w1_raw[(0, 1, 0)]
+        g01 = weight("w01", [("g", r, 128 * i, 32 * i, 32 * i + 32) for i in range(4)])
+        r = w1_raw[(1, 1, 0)]
+        g11 = weight("w11", [("g", r, 0, 0, 32), ("g", r, 128, 32, 64), ("v", r, 256, 64, 128)])
+        gb = [weight("wb%d" % b, [("g", wb_raw[b], 128 * i, 32 * i, 32 * i + 32) for i in range(4)]) for b in range(2)]
+
+        hq = {}
+
+        def stage1(b, jh):
+            hb = kt([P, 512, 4], BF16, "hb%d%d" % (b, jh))
+            for jq in range(4):
+                j0 = 512 * jh + P * jq
+                bank = ps1.tile([P, 4, P], F32, name="bank1")
+                for a in range(2):
+                    codes, scales = w1q[(a, b)]
+                    for t in range(4):
+                        nc.tensor.matmul_mx(out=bank[:, t, :], lhsT=codes[:, P * t : P * t + P].bitcast(FP8X4), lhsT_scale=scales[:, P * t : P * t + P],
+                                            rhs=vw[a][:, j0 : j0 + P].bitcast(FP8X4), rhs_scale=vs[4 * a : P, j0 : j0 + P],
+                                            start=(a == 0 and t == 0), stop=(a == 1 and t == 3))
+                lp = ring.tile([P, 4, P], F32, name="lp")
+                for t in range(4):
+                    nc.scalar.activation(out=lp[:, t, :], in_=bank[:, t, :], func=ACT.Copy, scale=leak_t[:, b, t : t + 1])
+                nc.vector.tensor_tensor(out=hb[:, P * jq : P * jq + P, :].rearrange("p (c i) t -> p c t i", i=2),
+                                        in0=bank[:].rearrange("p t (c i) -> p c t i", i=2),
+                                        in1=lp[:].rearrange("p t (c i) -> p c t i", i=2), op=ALU.max)
+            return hb
+
+        def hquant(hb, b, jh):
+            hq[(b, jh)] = quant(hb[:].rearrange("p j t -> p (j t)"), 512, "hq%d%d" % (b, jh))
+
+        e_t = [kt([P, S], F32, "e%d" % t) for t in range(4)]
+        d_t = [kt([P, S], F32, "d%d" % t) for t in range(4)]
+        wbq = {}
+
+        def e_part(t, jh):
+            bank = ps2.tile([P, 512], F32, name="bank2")
+            for b in range(2):
+                codes, scales = hq[(b, jh)]
+                nc.tensor.matmul_mx(out=bank[:], lhsT=waw[:, b, 256 * t : 256 * t + 256].bitcast(FP4X4), lhsT_scale=was[:, b, P * t : P * t + P],
+                                    rhs=codes[:].bitcast(FP8X4), rhs_scale=scales[:], start=(b == 0), stop=(b == 1))
+            nc.scalar.copy(out=e_t[t][:, 512 * jh : 512 * jh + 512], in_=bank[:])
+
+        def d_part(t, jh):
+            bank = ps2.tile([P, 512], F32, name="bank2")
+            for b in range(2):
+                codes, scales = hq[(b, jh)]
+                wc, ws = wbq[b]
+                nc.tensor.matmul_mx(out=bank[:], lhsT=wc[:, P * t : P * t + P].bitcast(FP8X4), lhsT_scale=ws[:, P * t : P * t + P],
+                                    rhs=codes[:].bitcast(FP8X4), rhs_scale=scales[:], start=(b == 0), stop=(b == 1))
+            cols = slice(512 * jh, 512 * jh + 512)
+            nc.vector.tensor_tensor(out=d_t[t][:, cols], in0=bank[:], in1=site_t[t][:, cols], op=ALU.add)
+
+        hb00 = stage1(0, 0)
+        w1q[(0, 1)] = wq(g01, "w01")
+        hb01 = stage1(0, 1)
+        w1q[(1, 1)] = wq(g11, "w11")
+        hquant(hb00, 0, 0)
+        hb10 = stage1(1, 0)
+        hquant(hb01, 0, 1)
+        hquant(hb10, 1, 0)
+        hb11 = stage1(1, 1)
+        wbq[0] = wq(gb[0], "wb0")
+        wbq[1] = wq(gb[1], "wb1")
+        hquant(hb11, 1, 1)
+        for t in range(4):
+            e_part(t, 0)
+            d_part(t, 0)
+
+        y = kt([P, 4, NP], F32, "y", "tabw0")
+        out_v = out_0.rearrange("(p t) m -> t p m", t=4)
+        for t in range(4):
+            d_part(t, 1)
+            e_part(t, 1)
+        yb = kt([P, NP, 4], BF16, "yb", "tabw1")
+        ycodes = kt([P, NP], U32, "ycodes")
+        yscales = kt([P, NP], U8, "yscales")
+        words_v = out_1[0].rearrange("p m t -> p (m t)").bitcast(I32)
+
+        def finish(t, m0, m1):
+            w = m1 - m0
+            c = ring.tile([P, w], F32, name="c")
+            gate = ring.tile([P, w], F32, name="gate")
+            z = ring.tile([P, w], F32, name="z")
+            lc = slice(m0 // 16, m1 // 16)
+            nc.vector.tensor_copy(out=c[:], in_=d_t[t][:].indirect(pos2_t[:, lc]))
+            nc.scalar.activation(out=gate[:], in_=e_t[t][:].indirect(pos1_t[:, lc]), func=ACT.Sigmoid, bias=thresh_t[:, t : t + 1], scale=steep_t[:, t : t + 1])
+            nc.vector.scalar_tensor_tensor(out=z[:], in0=gate[:], scalar=swing_t[:, t : t + 1], in1=c[:], op0=ALU.mult, op1=ALU.min)
+            nc.vector.tensor_tensor(out=y[:, t, m0:m1], in0=z[:], in1=c[:], op=ALU.add)
+            nc.sync.dma_start(out=out_v[t][:, m0:m1], in_=y[:, t, m0:m1])
+
+        def planes(m0, m1, on_scalar):
+            o = yb[:, m0:m1, :].rearrange("p (c i) t -> p c t i", i=4)
+            i_ = y[:, :, m0:m1].rearrange("p t (c i) -> p c t i", i=4)
+            if on_scalar:
+                nc.scalar.copy(out=o, in_=i_)
+            else:
+                nc.vector.tensor_copy(out=o, in_=i_)
+
+        def pquant(m0, m1):
+            nc.vector.quantize_mx(out=ycodes[:, m0:m1].bitcast(FP8X4), scales=yscales[:, m0:m1], in_=yb[:, m0:m1, :].rearrange("p m t -> p (m t)"))
+            nc.sync.dma_start(out=words_v[:, m0:m1], in_=ycodes[:, m0:m1].bitcast(I32))
+
+        for t in range(3):
+            finish(t, 0, 512)
+        finish(3, 0, 256)
+        planes(0, 256, True)
+        finish(3, 256, 512)
+        planes(256, 512, False)
+        pquant(0, 256)
+        pquant(256, 512)
+        for q in range(4):
+            eng = nc.scalar if q % 2 else nc.sync
+            eng.dma_start(out=out_2[0, 4 * q : 4 * q + 4, :].bitcast(I32), in_=yscales[32 * q : 32 * q + 4, :].bitcast(I32))

@@ -50,31 +50,39 @@ def tile_list_roaming_gate_scores_kernel(tc, tab_words, tab_scales, offs, pos1, 
         nc.vector.memset(tabs[:].bitcast(I32), 0)
         nc.vector.memset(was_raw[:].bitcast(I32), 0)
 
-        nc.sync.dma_start(offs_t[:], offs)
-        for a in range(2):
+        def load_tab(a):
             nc.sync.dma_start(out=tabw[a][:], in_=tab_words[a].rearrange("p t i -> p (t i)").bitcast(I32))
-        for q in range(4):
-            nc.gpsimd.dma_start(out=tabs[32 * q : 32 * q + 8, :].bitcast(I32), in_=tab_scales[:, 4 * q : 4 * q + 4, :].bitcast(I32))
-        leak_t = kt([P, 2, 4], F32, "leak_t")
-        nc.gpsimd.dma_start(out=leak_t[:], in_=leak.rearrange("(b p t) -> p b t", b=2, t=4))
-        for q in range(4):
-            nc.gpsimd.dma_start(out=was_raw[32 * q : 32 * q + 4].bitcast(I32), in_=wa_scales[:, 4 * q : 4 * q + 4, :].rearrange("a r c -> r a c").bitcast(I32))
-        vecs = []
-        for nm, v in (("steep_t", steep), ("thresh_t", thresh), ("swing_t", swing)):
-            vt = kt([P, 4], F32, nm)
-            nc.gpsimd.dma_start(out=vt[:], in_=v.rearrange("(p t) -> p t", t=4))
-            vecs.append(vt)
-        steep_t, thresh_t, swing_t = vecs
-        nc.sync.dma_start(out=waw_raw[:].bitcast(I32), in_=wa_words.rearrange("a p c -> p a c").bitcast(I32))
 
         w1_raw = {}
-        for a, b, halves in ((0, 0, 1), (1, 0, 2), (0, 1, 1), (1, 1, 1)):
+
+        def load_w1(a, b, hf, halves):
             w = 512 // halves
-            for hf in range(halves):
-                r = kt([P, 4, w], F32, "w1r%d%d%d" % (a, b, hf))
-                c0 = 512 * b + w * hf
-                nc.sync.dma_start(out=r[:], in_=w1[512 * a : 512 * a + 512, c0 : c0 + w].rearrange("(p j) c -> p j c", j=4))
-                w1_raw[(a, b, hf)] = r
+            r = kt([P, 4, w], F32, "w1r%d%d%d" % (a, b, hf))
+            c0 = 512 * b + w * hf
+            nc.sync.dma_start(out=r[:], in_=w1[512 * a : 512 * a + 512, c0 : c0 + w].rearrange("(p j) c -> p j c", j=4))
+            w1_raw[(a, b, hf)] = r
+
+        def load_vec(v, nm):
+            vt = kt([P, 4], F32, nm)
+            nc.sync.dma_start(out=vt[:], in_=v.rearrange("(p t) -> p t", t=4))
+            return vt
+
+        stage = kt([P, T // 4], I32, "stage")
+        nc.sync.dma_start(offs_t[:], offs)
+        for q in range(4):
+            nc.sync.dma_start(out=stage[32 * q : 32 * q + 8, :], in_=tab_scales[:, 4 * q : 4 * q + 4, :].bitcast(I32))
+        load_tab(0)
+        nc.sync.dma_start(out=waw_raw[:].bitcast(I32), in_=wa_words.rearrange("a p c -> p a c").bitcast(I32))
+        load_tab(1)
+        load_w1(0, 0, 0, 1)
+        load_w1(1, 0, 0, 2)
+        load_w1(1, 0, 1, 2)
+        leak_t = kt([P, 2, 4], F32, "leak_t")
+        nc.sync.dma_start(out=leak_t[:], in_=leak.rearrange("(b p t) -> p b t", b=2, t=4))
+        for q in range(4):
+            nc.sync.dma_start(out=was_raw[32 * q : 32 * q + 4].bitcast(I32), in_=wa_scales[:, 4 * q : 4 * q + 4, :].rearrange("a r c -> r a c").bitcast(I32))
+        load_w1(0, 1, 0, 1)
+        load_w1(1, 1, 0, 1)
         wb_raw = []
         for b in range(2):
             r = kt([P, 4, N], F32, "wbr%d" % b)
@@ -82,28 +90,34 @@ def tile_list_roaming_gate_scores_kernel(tc, tab_words, tab_scales, offs, pos1, 
             wb_raw.append(r)
         nc.sync.dma_start(pos1_t[:], pos1)
         nc.sync.dma_start(pos2_t[:], pos2)
+        steep_t = load_vec(steep, "steep_t")
+        thresh_t = load_vec(thresh, "thresh_t")
+        swing_t = load_vec(swing, "swing_t")
         site_v = site.rearrange("(p t) j -> t p j", t=4)
         site_t = []
         for t in range(4):
-            r = kt([P, S], F32, "site%d" % t, ("w1r000", "w1r100", "w1r101", None)[t])
+            r = kt([P, S], F32, "site%d" % t, ("w1r000", "w1r100", "w1r101", "stage")[t])
             nc.sync.dma_start(out=r[:], in_=site_v[t])
             site_t.append(r)
 
+        for q in range(4):
+            nc.vector.tensor_copy(out=tabs[32 * q : 32 * q + 8, :].bitcast(I32), in_=stage[32 * q : 32 * q + 8, :])
+        waw = kt([P, 2, 2 * N], U8, "waw")
         vs = kt([P, S], U8, "vs")
         nc.vector.tensor_copy(out=vs[:], in_=tabs[:].indirect(offs_t[:]))
+        nc.vector.tensor_copy(out=waw[:].rearrange("p a c -> p (a c)").bitcast(U16).rearrange("p (a t m) -> p a t m", a=2, t=4),
+                              in_=waw_raw[:].rearrange("p a c -> p (a c)").bitcast(U16).rearrange("p (a m t) -> p a t m", a=2, t=4))
         vw = [kt([P, S], U32, "vw%d" % a) for a in range(2)]
         nc.vector.tensor_copy(out=vw[0][:], in_=tabw[0][:].bitcast(U32).indirect(offs_t[:]))
-        waw = kt([P, 2, 2 * N], U8, "waw")
         was = kt([P, 2, N], U8, "was")
-        for a in range(2):
-            nc.vector.tensor_copy(out=waw[:, a, :].rearrange("p (t m e) -> p t m e", t=4, e=2), in_=waw_raw[:, a, :].rearrange("p (m t e) -> p t m e", t=4, e=2))
-        nc.vector.tensor_copy(out=was[:].rearrange("p a (t m) -> p a t m", t=4), in_=was_raw[:].rearrange("p a (m t) -> p a t m", t=4))
         nc.vector.tensor_copy(out=vw[1][:], in_=tabw[1][:].bitcast(U32).indirect(offs_t[:]))
 
-        def quant(src, width, name):
+        def quant(src, width, name, parts=1):
             codes = kt([P, width], U32, name + "_c")
             scales = kt([P, width], U8, name + "_s")
-            nc.vector.quantize_mx(out=codes[:].bitcast(FP8X4), scales=scales[:], in_=src)
+            w = width // parts
+            for i in range(parts):
+                nc.vector.quantize_mx(out=codes[:, w * i : w * i + w].bitcast(FP8X4), scales=scales[:, w * i : w * i + w], in_=src[:, 4 * w * i : 4 * w * (i + 1)])
             return codes, scales
 
         def weight(name, pieces):
@@ -112,20 +126,14 @@ def tile_list_roaming_gate_scores_kernel(tc, tab_words, tab_scales, offs, pos1, 
                 cast(nc, eng, g, raw[:, :, c0 : c0 + 4 * (m1 - m0)], m0, m1)
             return g
 
-        def wq(g, name):
-            return quant(g[:].rearrange("p t m j -> p (t m j)"), 512, name)
+        def wq(g, name, parts=1):
+            return quant(g[:].rearrange("p t m j -> p (t m j)"), 512, name, parts)
 
         w1q = {}
         r = w1_raw[(0, 0, 0)]
         w1q[(0, 0)] = wq(weight("w00", [("s", r, 0, 0, 48), ("v", r, 192, 48, 128)]), "w00")
         r0, r1 = w1_raw[(1, 0, 0)], w1_raw[(1, 0, 1)]
-        w1q[(1, 0)] = wq(weight("w10", [("s", r0, 0, 0, 64), ("s", r1, 0, 64, 80), ("v", r1, 64, 80, 128)]), "w10")
-        r = w1_raw[(0, 1, 0)]
-        g01 = weight("w01", [("g", r, 128 * i, 32 * i, 32 * i + 32) for i in range(4)])
-        r = w1_raw[(1, 1, 0)]
-        g11 = weight("w11", [("g", r, 0, 0, 32), ("g", r, 128, 32, 64), ("v", r, 256, 64, 128)])
-        gb = [weight("wb%d" % b, [("g", wb_raw[b], 128 * i, 32 * i, 32 * i + 32) for i in range(4)]) for b in range(2)]
-
+        w1q[(1, 0)] = wq(weight("w10", [("s", r0, 0, 0, 64), ("s", r1, 0, 64, 80), ("v", r1, 64, 80, 128)]), "w10", 2)
         hq = {}
 
         def stage1(b, jh):
@@ -172,21 +180,29 @@ def tile_list_roaming_gate_scores_kernel(tc, tab_words, tab_scales, offs, pos1, 
             cols = slice(512 * jh, 512 * jh + 512)
             nc.vector.tensor_tensor(out=d_t[t][:, cols], in0=bank[:], in1=site_t[t][:, cols], op=ALU.add)
 
+        def quarters(name, raw, engines):
+            return weight(name, [(engines[i], raw, 128 * i, 32 * i, 32 * i + 32) for i in range(4)])
+
         hb00 = stage1(0, 0)
+        g01 = quarters("w01", w1_raw[(0, 1, 0)], "ssvv")
+        hquant(hb00, 0, 0)
         w1q[(0, 1)] = wq(g01, "w01")
+        g11 = quarters("w11", w1_raw[(1, 1, 0)], "vvvv")
         hb01 = stage1(0, 1)
         w1q[(1, 1)] = wq(g11, "w11")
-        hquant(hb00, 0, 0)
         hb10 = stage1(1, 0)
         hquant(hb01, 0, 1)
+        gb0 = quarters("wb0", wb_raw[0], "sssv")
         hquant(hb10, 1, 0)
+        gb1 = quarters("wb1", wb_raw[1], "ssvv")
         hb11 = stage1(1, 1)
-        wbq[0] = wq(gb[0], "wb0")
-        wbq[1] = wq(gb[1], "wb1")
+        wbq[0] = wq(gb0, "wb0")
+        wbq[1] = wq(gb1, "wb1")
         hquant(hb11, 1, 1)
+        nc.vector.tensor_copy(out=was[:].rearrange("p a (t m) -> p a t m", t=4), in_=was_raw[:].rearrange("p a (m t) -> p a t m", t=4))
         for t in range(4):
-            e_part(t, 0)
             d_part(t, 0)
+            e_part(t, 0)
 
         y = kt([P, 4, NP], F32, "y", "tabw0")
         out_v = out_0.rearrange("(p t) m -> t p m", t=4)

@@ -18,15 +18,13 @@ FLOPS = 2 * K * H * S + 2 * 2 * H * N * S
 P = 128
 
 
-def cast(nc, eng, dst, raw, m0, m1):
-    o = dst[:].rearrange("p t m j -> p m t j")[:, m0:m1]
-    i = raw.rearrange("p j (m t) -> p m t j", t=4)
+def cast(nc, eng, dst, raw, tp, m0, m1):
+    o = dst[:, 2 * tp : 2 * tp + 2, m0:m1, :].rearrange("p t m j -> p m j t")
+    i = raw.rearrange("p j (m t) -> p m j t", t=4)[:, :, :, 2 * tp : 2 * tp + 2]
     if eng == "v":
         nc.vector.tensor_copy(out=o, in_=i)
-    elif eng == "s":
-        nc.scalar.copy(out=o, in_=i)
     else:
-        nc.gpsimd.tensor_scalar(out=o, in0=i, scalar1=1.0, scalar2=0.0, op0=ALU.mult, op1=ALU.add)
+        nc.scalar.copy(out=o, in_=i)
 
 
 def tile_list_roaming_gate_scores_kernel(tc, tab_words, tab_scales, offs, pos1, pos2, w1, leak, wa_words, wa_scales, wb, site, steep, thresh, swing, out_0, out_1, out_2):
@@ -69,9 +67,18 @@ def tile_list_roaming_gate_scores_kernel(tc, tab_words, tab_scales, offs, pos1, 
 
         stage = kt([P, T // 4], I32, "stage")
         nc.sync.dma_start(offs_t[:], offs)
-        for q in range(4):
-            nc.sync.dma_start(out=stage[32 * q : 32 * q + 8, :], in_=tab_scales[:, 4 * q : 4 * q + 4, :].bitcast(I32))
-        load_tab(0)
+        tab0 = tab_words[0].rearrange("p t i -> p (t i)").bitcast(I32)
+
+        def load_scale(i):
+            a, q = i % 2, i // 2
+            nc.sync.dma_start(out=stage[32 * q + 4 * a : 32 * q + 4 * a + 4, :], in_=tab_scales[a, 4 * q : 4 * q + 4, :].bitcast(I32))
+
+        for i in range(6):
+            load_scale(i)
+        nc.sync.dma_start(out=tabw[0][:, : T // 2], in_=tab0[:, : T // 2])
+        load_scale(6)
+        load_scale(7)
+        nc.sync.dma_start(out=tabw[0][:, T // 2 :], in_=tab0[:, T // 2 :])
         nc.sync.dma_start(out=waw_raw[:].bitcast(I32), in_=wa_words.rearrange("a p c -> p a c").bitcast(I32))
         load_tab(1)
         load_w1(0, 0, 0, 1)
@@ -122,8 +129,8 @@ def tile_list_roaming_gate_scores_kernel(tc, tab_words, tab_scales, offs, pos1, 
 
         def weight(name, pieces):
             g = kt([P, 4, P, 4], BF16, name + "_g")
-            for eng, raw, c0, m0, m1 in pieces:
-                cast(nc, eng, g, raw[:, :, c0 : c0 + 4 * (m1 - m0)], m0, m1)
+            for eng, raw, c0, tp, m0, m1 in pieces:
+                cast(nc, eng, g, raw[:, :, c0 : c0 + 4 * (m1 - m0)], tp, m0, m1)
             return g
 
         def wq(g, name, parts=1):
@@ -131,9 +138,9 @@ def tile_list_roaming_gate_scores_kernel(tc, tab_words, tab_scales, offs, pos1, 
 
         w1q = {}
         r = w1_raw[(0, 0, 0)]
-        w1q[(0, 0)] = wq(weight("w00", [("s", r, 0, 0, 48), ("v", r, 192, 48, 128)]), "w00")
+        w1q[(0, 0)] = wq(weight("w00", [("s", r, 0, 0, 0, 128), ("v", r, 0, 1, 0, 128)]), "w00")
         r0, r1 = w1_raw[(1, 0, 0)], w1_raw[(1, 0, 1)]
-        w1q[(1, 0)] = wq(weight("w10", [("s", r0, 0, 0, 64), ("s", r1, 0, 64, 80), ("v", r1, 64, 80, 128)]), "w10", 2)
+        w1q[(1, 0)] = wq(weight("w10", [("v", r0, 0, 0, 0, 64), ("s", r0, 0, 1, 0, 64), ("v", r1, 0, 0, 64, 128), ("s", r1, 0, 1, 64, 128)]), "w10", 2)
         hq = {}
 
         def stage1(b, jh):
@@ -181,20 +188,20 @@ def tile_list_roaming_gate_scores_kernel(tc, tab_words, tab_scales, offs, pos1, 
             nc.vector.tensor_tensor(out=d_t[t][:, cols], in0=bank[:], in1=site_t[t][:, cols], op=ALU.add)
 
         def quarters(name, raw, engines):
-            return weight(name, [(engines[i], raw, 128 * i, 32 * i, 32 * i + 32) for i in range(4)])
+            return weight(name, [(engines[i], raw, 256 * (i % 2), i // 2, 64 * (i % 2), 64 * (i % 2) + 64) for i in range(4)])
 
         hb00 = stage1(0, 0)
         g01 = quarters("w01", w1_raw[(0, 1, 0)], "ssvv")
         hquant(hb00, 0, 0)
         w1q[(0, 1)] = wq(g01, "w01")
-        g11 = quarters("w11", w1_raw[(1, 1, 0)], "vvvv")
+        g11 = quarters("w11", w1_raw[(1, 1, 0)], "ssvv")
         hb01 = stage1(0, 1)
         w1q[(1, 1)] = wq(g11, "w11")
         hb10 = stage1(1, 0)
         hquant(hb01, 0, 1)
         gb0 = quarters("wb0", wb_raw[0], "sssv")
         hquant(hb10, 1, 0)
-        gb1 = quarters("wb1", wb_raw[1], "ssvv")
+        gb1 = quarters("wb1", wb_raw[1], "sssv")
         hb11 = stage1(1, 1)
         wbq[0] = wq(gb0, "wb0")
         wbq[1] = wq(gb1, "wb1")
@@ -206,29 +213,36 @@ def tile_list_roaming_gate_scores_kernel(tc, tab_words, tab_scales, offs, pos1, 
 
         y = kt([P, 4, NP], F32, "y", "tabw0")
         out_v = out_0.rearrange("(p t) m -> t p m", t=4)
-        for t in range(4):
-            d_part(t, 1)
-            e_part(t, 1)
         yb = kt([P, NP, 4], BF16, "yb", "tabw1")
         ycodes = kt([P, NP], U32, "ycodes")
         yscales = kt([P, NP], U8, "yscales")
         words_v = out_1[0].rearrange("p m t -> p (m t)").bitcast(I32)
 
-        def finish(t, m0, m1):
+        picked = {}
+
+        def pick(t, m0, m1):
             w = m1 - m0
             c = ring.tile([P, w], F32, name="c")
             gate = ring.tile([P, w], F32, name="gate")
-            z = ring.tile([P, w], F32, name="z")
             lc = slice(m0 // 16, m1 // 16)
             nc.vector.tensor_copy(out=c[:], in_=d_t[t][:].indirect(pos2_t[:, lc]))
             nc.scalar.activation(out=gate[:], in_=e_t[t][:].indirect(pos1_t[:, lc]), func=ACT.Sigmoid, bias=thresh_t[:, t : t + 1], scale=steep_t[:, t : t + 1])
+            picked[(t, m0)] = [c, gate]
+
+        def cap(t, m0, m1):
+            c, gate = picked[(t, m0)]
+            z = ring.tile([P, m1 - m0], F32, name="z")
             nc.vector.scalar_tensor_tensor(out=z[:], in0=gate[:], scalar=swing_t[:, t : t + 1], in1=c[:], op0=ALU.mult, op1=ALU.min)
+            picked[(t, m0)].append(z)
+
+        def total(t, m0, m1):
+            c, gate, z = picked[(t, m0)]
             nc.vector.tensor_tensor(out=y[:, t, m0:m1], in0=z[:], in1=c[:], op=ALU.add)
             nc.sync.dma_start(out=out_v[t][:, m0:m1], in_=y[:, t, m0:m1])
 
         def planes(m0, m1, on_scalar):
-            o = yb[:, m0:m1, :].rearrange("p (c i) t -> p c t i", i=4)
-            i_ = y[:, :, m0:m1].rearrange("p t (c i) -> p c t i", i=4)
+            o = yb[:, m0:m1, :].rearrange("p (c i) t -> p c t i", i=2)
+            i_ = y[:, :, m0:m1].rearrange("p t (c i) -> p c t i", i=2)
             if on_scalar:
                 nc.scalar.copy(out=o, in_=i_)
             else:
@@ -238,11 +252,19 @@ def tile_list_roaming_gate_scores_kernel(tc, tab_words, tab_scales, offs, pos1, 
             nc.vector.quantize_mx(out=ycodes[:, m0:m1].bitcast(FP8X4), scales=yscales[:, m0:m1], in_=yb[:, m0:m1, :].rearrange("p m t -> p (m t)"))
             nc.sync.dma_start(out=words_v[:, m0:m1], in_=ycodes[:, m0:m1].bitcast(I32))
 
-        for t in range(3):
-            finish(t, 0, 512)
-        finish(3, 0, 256)
-        planes(0, 256, True)
-        finish(3, 256, 512)
+        units = [(0, 0, 512), (1, 0, 512), (2, 0, 512), (3, 0, 256), (3, 256, 512)]
+        for step in range(len(units) + 3):
+            if step < 4:
+                e_part(step, 1)
+                d_part(step, 1)
+            if 3 <= step:
+                total(*units[step - 3])
+            if 1 <= step <= len(units):
+                pick(*units[step - 1])
+            if 2 <= step <= len(units) + 1:
+                cap(*units[step - 2])
+            if step == len(units) + 1:
+                planes(0, 256, True)
         planes(256, 512, False)
         pquant(0, 256)
         pquant(256, 512)

@@ -16,15 +16,22 @@ ACT = mybir.ActivationFunctionType
 K, T, S, NP, H, N = 1024, 4096, 1024, 512, 1024, 512
 FLOPS = 2 * K * H * S + 2 * 2 * H * N * S
 P = 128
+PASS = 512
+HALF_M = P // 2
+HALF_NP = NP // 2
+LIST = 16
+
+W1_LATE_SHARE = "ssvv"
+WB_SHARE = "sssv"
 
 
-def cast(nc, eng, dst, raw, tp, m0, m1):
-    o = dst[:, 2 * tp : 2 * tp + 2, m0:m1, :].rearrange("p t m j -> p m j t")
-    i = raw.rearrange("p j (m t) -> p m j t", t=4)[:, :, :, 2 * tp : 2 * tp + 2]
-    if eng == "v":
-        nc.vector.tensor_copy(out=o, in_=i)
+def cast_piece(nc, engine, dealt, raw, pair, m0, m1):
+    dst = dealt[:, 2 * pair : 2 * pair + 2, m0:m1, :].rearrange("p t m i -> p m i t")
+    src = raw.rearrange("p i (m t) -> p m i t", t=4)[:, :, :, 2 * pair : 2 * pair + 2]
+    if engine == "v":
+        nc.vector.tensor_copy(out=dst, in_=src)
     else:
-        nc.scalar.copy(out=o, in_=i)
+        nc.scalar.copy(out=dst, in_=src)
 
 
 def tile_list_roaming_gate_scores_kernel(tc, tab_words, tab_scales, offs, pos1, pos2, w1, leak, wa_words, wa_scales, wb, site, steep, thresh, swing, out_0, out_1, out_2):
@@ -32,242 +39,237 @@ def tile_list_roaming_gate_scores_kernel(tc, tab_words, tab_scales, offs, pos1, 
     with ExitStack() as ctx:
         keep = ctx.enter_context(tc.tile_pool(name="keep", bufs=1))
         ring = ctx.enter_context(tc.tile_pool(name="ring", bufs=3))
-        ps1 = ctx.enter_context(tc.psum_pool(name="ps1", bufs=4))
-        ps2 = ctx.enter_context(tc.psum_pool(name="ps2", bufs=4))
+        psum = ctx.enter_context(tc.psum_pool(name="psum", bufs=8))
 
-        def kt(shape, dt, name, tag=None):
-            return keep.tile(shape, dt, name=name, tag=tag or name, align_bytes=64)
+        def kept(shape, dtype, name, tag=None):
+            return keep.tile(shape, dtype, name=name, tag=tag or name, align_bytes=64)
 
-        offs_t = keep.tile([P, S // 16], U16, name="offs_t")
-        pos1_t = keep.tile([P, NP // 16], U16, name="pos1_t")
-        pos2_t = keep.tile([P, NP // 16], U16, name="pos2_t")
-        tabw = [kt([P, T], I32, "tabw%d" % a) for a in range(2)]
-        tabs = kt([P, T], U8, "tabs")
-        was_raw = kt([P, 2, N], U8, "was_raw")
-        waw_raw = kt([P, 2, 2 * N], U8, "waw_raw")
-        nc.vector.memset(tabs[:].bitcast(I32), 0)
-        nc.vector.memset(was_raw[:].bitcast(I32), 0)
-
-        def load_tab(a):
-            nc.sync.dma_start(out=tabw[a][:], in_=tab_words[a].rearrange("p t i -> p (t i)").bitcast(I32))
+        offs_t = keep.tile([P, S // LIST], U16, name="offs_t")
+        pos1_t = keep.tile([P, NP // LIST], U16, name="pos1_t")
+        pos2_t = keep.tile([P, NP // LIST], U16, name="pos2_t")
+        table_words = [kept([P, T], I32, "table_words%d" % a) for a in range(2)]
+        table_scales = kept([P, T], U8, "table_scales")
+        wa_scales_raw = kept([P, 2, N], U8, "wa_scales_raw")
+        wa_words_raw = kept([P, 2, 2 * N], U8, "wa_words_raw")
+        nc.vector.memset(table_scales[:].bitcast(I32), 0)
+        nc.vector.memset(wa_scales_raw[:].bitcast(I32), 0)
 
         w1_raw = {}
 
-        def load_w1(a, b, hf, halves):
-            w = 512 // halves
-            r = kt([P, 4, w], F32, "w1r%d%d%d" % (a, b, hf))
-            c0 = 512 * b + w * hf
-            nc.sync.dma_start(out=r[:], in_=w1[512 * a : 512 * a + 512, c0 : c0 + w].rearrange("(p j) c -> p j c", j=4))
-            w1_raw[(a, b, hf)] = r
+        def load_w1(a, b, part, parts):
+            width = PASS // parts
+            raw = kept([P, 4, width], F32, "w1_raw%d%d%d" % (a, b, part))
+            c0 = PASS * b + width * part
+            nc.sync.dma_start(out=raw[:], in_=w1[PASS * a : PASS * (a + 1), c0 : c0 + width].rearrange("(p i) c -> p i c", i=4))
+            w1_raw[(a, b, part)] = raw
 
-        def load_vec(v, nm):
-            vt = kt([P, 4], F32, nm)
-            nc.sync.dma_start(out=vt[:], in_=v.rearrange("(p t) -> p t", t=4))
-            return vt
+        def load_rows(values, name):
+            dealt = kept([P, 4], F32, name)
+            nc.sync.dma_start(out=dealt[:], in_=values.rearrange("(p t) -> p t", t=4))
+            return dealt
 
-        stage = kt([P, T // 4], I32, "stage")
+        scale_stage = kept([P, T // 4], I32, "scale_stage")
+
+        def load_scale_rows(quadrant):
+            for a in range(2):
+                row = 32 * quadrant + 4 * a
+                nc.sync.dma_start(out=scale_stage[row : row + 4, :], in_=tab_scales[a, 4 * quadrant : 4 * quadrant + 4, :].bitcast(I32))
+
+        words_in = [tab_words[a].rearrange("p c i -> p (c i)").bitcast(I32) for a in range(2)]
         nc.sync.dma_start(offs_t[:], offs)
-        tab0 = tab_words[0].rearrange("p t i -> p (t i)").bitcast(I32)
-
-        def load_scale(i):
-            a, q = i % 2, i // 2
-            nc.sync.dma_start(out=stage[32 * q + 4 * a : 32 * q + 4 * a + 4, :], in_=tab_scales[a, 4 * q : 4 * q + 4, :].bitcast(I32))
-
-        for i in range(6):
-            load_scale(i)
-        nc.sync.dma_start(out=tabw[0][:, : T // 2], in_=tab0[:, : T // 2])
-        load_scale(6)
-        load_scale(7)
-        nc.sync.dma_start(out=tabw[0][:, T // 2 :], in_=tab0[:, T // 2 :])
-        nc.sync.dma_start(out=waw_raw[:].bitcast(I32), in_=wa_words.rearrange("a p c -> p a c").bitcast(I32))
-        load_tab(1)
+        for quadrant in range(3):
+            load_scale_rows(quadrant)
+        nc.sync.dma_start(out=table_words[0][:, : T // 2], in_=words_in[0][:, : T // 2])
+        load_scale_rows(3)
+        nc.sync.dma_start(out=table_words[0][:, T // 2 :], in_=words_in[0][:, T // 2 :])
+        nc.sync.dma_start(out=wa_words_raw[:].bitcast(I32), in_=wa_words.rearrange("a p c -> p a c").bitcast(I32))
+        for quadrant in range(4):
+            nc.sync.dma_start(out=wa_scales_raw[32 * quadrant : 32 * quadrant + 4].bitcast(I32),
+                              in_=wa_scales[:, 4 * quadrant : 4 * quadrant + 4, :].rearrange("a r c -> r a c").bitcast(I32))
+        nc.sync.dma_start(out=table_words[1][:], in_=words_in[1])
         load_w1(0, 0, 0, 1)
         load_w1(1, 0, 0, 2)
         load_w1(1, 0, 1, 2)
-        leak_t = kt([P, 2, 4], F32, "leak_t")
+        leak_t = kept([P, 2, 4], F32, "leak_t")
         nc.sync.dma_start(out=leak_t[:], in_=leak.rearrange("(b p t) -> p b t", b=2, t=4))
-        for q in range(4):
-            nc.sync.dma_start(out=was_raw[32 * q : 32 * q + 4].bitcast(I32), in_=wa_scales[:, 4 * q : 4 * q + 4, :].rearrange("a r c -> r a c").bitcast(I32))
         load_w1(0, 1, 0, 1)
         load_w1(1, 1, 0, 1)
         wb_raw = []
         for b in range(2):
-            r = kt([P, 4, N], F32, "wbr%d" % b)
-            nc.sync.dma_start(out=r[:], in_=wb[512 * b : 512 * b + 512, :].rearrange("(p j) c -> p j c", j=4))
-            wb_raw.append(r)
+            raw = kept([P, 4, N], F32, "wb_raw%d" % b)
+            nc.sync.dma_start(out=raw[:], in_=wb[PASS * b : PASS * (b + 1), :].rearrange("(p i) c -> p i c", i=4))
+            wb_raw.append(raw)
         nc.sync.dma_start(pos1_t[:], pos1)
         nc.sync.dma_start(pos2_t[:], pos2)
-        steep_t = load_vec(steep, "steep_t")
-        thresh_t = load_vec(thresh, "thresh_t")
-        swing_t = load_vec(swing, "swing_t")
-        site_v = site.rearrange("(p t) j -> t p j", t=4)
+        steep_t = load_rows(steep, "steep_t")
+        thresh_t = load_rows(thresh, "thresh_t")
+        swing_t = load_rows(swing, "swing_t")
+        site_rows = site.rearrange("(p t) j -> t p j", t=4)
         site_t = []
-        for t in range(4):
-            r = kt([P, S], F32, "site%d" % t, ("w1r000", "w1r100", "w1r101", "stage")[t])
-            nc.sync.dma_start(out=r[:], in_=site_v[t])
-            site_t.append(r)
+        for t, spent in enumerate(("w1_raw000", "w1_raw100", "w1_raw101", "scale_stage")):
+            rows = kept([P, S], F32, "site%d" % t, spent)
+            nc.sync.dma_start(out=rows[:], in_=site_rows[t])
+            site_t.append(rows)
 
-        for q in range(4):
-            nc.vector.tensor_copy(out=tabs[32 * q : 32 * q + 8, :].bitcast(I32), in_=stage[32 * q : 32 * q + 8, :])
-        waw = kt([P, 2, 2 * N], U8, "waw")
-        vs = kt([P, S], U8, "vs")
-        nc.vector.tensor_copy(out=vs[:], in_=tabs[:].indirect(offs_t[:]))
-        nc.vector.tensor_copy(out=waw[:].rearrange("p a c -> p (a c)").bitcast(U16).rearrange("p (a t m) -> p a t m", a=2, t=4),
-                              in_=waw_raw[:].rearrange("p a c -> p (a c)").bitcast(U16).rearrange("p (a m t) -> p a t m", a=2, t=4))
-        vw = [kt([P, S], U32, "vw%d" % a) for a in range(2)]
-        nc.vector.tensor_copy(out=vw[0][:], in_=tabw[0][:].bitcast(U32).indirect(offs_t[:]))
-        was = kt([P, 2, N], U8, "was")
-        nc.vector.tensor_copy(out=vw[1][:], in_=tabw[1][:].bitcast(U32).indirect(offs_t[:]))
+        for quadrant in range(4):
+            live = slice(32 * quadrant, 32 * quadrant + 8)
+            nc.vector.tensor_copy(out=table_scales[live, :].bitcast(I32), in_=scale_stage[live, :])
+        wa_w = kept([P, 2, 2 * N], U8, "wa_w")
+        v_scales = kept([P, S], U8, "v_scales")
+        nc.vector.tensor_copy(out=v_scales[:], in_=table_scales[:].indirect(offs_t[:]))
+        nc.vector.tensor_copy(out=wa_w[:].rearrange("p a c -> p (a c)").bitcast(U16).rearrange("p (a t m) -> p a t m", a=2, t=4),
+                              in_=wa_words_raw[:].rearrange("p a c -> p (a c)").bitcast(U16).rearrange("p (a m t) -> p a t m", a=2, t=4))
+        v_words = [kept([P, S], U32, "v_words%d" % a) for a in range(2)]
+        nc.vector.tensor_copy(out=v_words[0][:], in_=table_words[0][:].bitcast(U32).indirect(offs_t[:]))
+        wa_s = kept([P, 2, N], U8, "wa_s")
+        nc.vector.tensor_copy(out=wa_s[:].rearrange("p a (t m) -> p a t m", t=4), in_=wa_scales_raw[:].rearrange("p a (m t) -> p a t m", t=4))
+        nc.vector.tensor_copy(out=v_words[1][:], in_=table_words[1][:].bitcast(U32).indirect(offs_t[:]))
 
-        def quant(src, width, name, parts=1):
-            codes = kt([P, width], U32, name + "_c")
-            scales = kt([P, width], U8, name + "_s")
-            w = width // parts
-            for i in range(parts):
-                nc.vector.quantize_mx(out=codes[:, w * i : w * i + w].bitcast(FP8X4), scales=scales[:, w * i : w * i + w], in_=src[:, 4 * w * i : 4 * w * (i + 1)])
+        def quantise(values, name, parts=1):
+            codes = kept([P, PASS], U32, name + "_codes")
+            scales = kept([P, PASS], U8, name + "_scales")
+            width = PASS // parts
+            for part in range(parts):
+                cols = slice(width * part, width * (part + 1))
+                nc.vector.quantize_mx(out=codes[:, cols].bitcast(FP8X4), scales=scales[:, cols], in_=values[:, 4 * cols.start : 4 * cols.stop])
             return codes, scales
 
-        def weight(name, pieces):
-            g = kt([P, 4, P, 4], BF16, name + "_g")
-            for eng, raw, c0, tp, m0, m1 in pieces:
-                cast(nc, eng, g, raw[:, :, c0 : c0 + 4 * (m1 - m0)], tp, m0, m1)
-            return g
+        def cast_weight(name, pieces):
+            dealt = kept([P, 4, P, 4], BF16, name + "_dealt")
+            for engine, raw, c0, pair, m0, m1 in pieces:
+                cast_piece(nc, engine, dealt, raw[:, :, c0 : c0 + 4 * (m1 - m0)], pair, m0, m1)
+            return dealt
 
-        def wq(g, name, parts=1):
-            return quant(g[:].rearrange("p t m j -> p (t m j)"), 512, name, parts)
+        def cast_quarters(name, raw, share):
+            return cast_weight(name, [(share[2 * pair + half], raw, 4 * HALF_M * half, pair, HALF_M * half, HALF_M * (half + 1))
+                                      for pair in range(2) for half in range(2)])
 
-        w1q = {}
-        r = w1_raw[(0, 0, 0)]
-        w1q[(0, 0)] = wq(weight("w00", [("s", r, 0, 0, 0, 128), ("v", r, 0, 1, 0, 128)]), "w00")
-        r0, r1 = w1_raw[(1, 0, 0)], w1_raw[(1, 0, 1)]
-        w1q[(1, 0)] = wq(weight("w10", [("v", r0, 0, 0, 0, 64), ("s", r0, 0, 1, 0, 64), ("v", r1, 0, 0, 64, 128), ("s", r1, 0, 1, 64, 128)]), "w10", 2)
-        hq = {}
+        def quantise_weight(dealt, name, parts=1):
+            return quantise(dealt[:].rearrange("p t m i -> p (t m i)"), name, parts)
 
-        def stage1(b, jh):
-            hb = kt([P, 512, 4], BF16, "hb%d%d" % (b, jh))
+        w1_q = {}
+        raw = w1_raw[(0, 0, 0)]
+        w1_q[(0, 0)] = quantise_weight(cast_weight("w1_00", [("s", raw, 0, 0, 0, P), ("v", raw, 0, 1, 0, P)]), "w1_00")
+        pieces = [(engine, w1_raw[(1, 0, half)], 0, pair, HALF_M * half, HALF_M * (half + 1)) for half in range(2) for pair, engine in enumerate("vs")]
+        w1_q[(1, 0)] = quantise_weight(cast_weight("w1_10", pieces), "w1_10", 2)
+
+        h_q = {}
+
+        def first_stage(b, jh):
+            h_bf = kept([P, PASS, 4], BF16, "h_bf%d%d" % (b, jh))
             for jq in range(4):
-                j0 = 512 * jh + P * jq
-                bank = ps1.tile([P, 4, P], F32, name="bank1")
+                j0 = PASS * jh + P * jq
+                bank = psum.tile([P, 4, P], F32, name="bank_h", tag="bank")
                 for a in range(2):
-                    codes, scales = w1q[(a, b)]
+                    codes, scales = w1_q[(a, b)]
                     for t in range(4):
-                        nc.tensor.matmul_mx(out=bank[:, t, :], lhsT=codes[:, P * t : P * t + P].bitcast(FP8X4), lhsT_scale=scales[:, P * t : P * t + P],
-                                            rhs=vw[a][:, j0 : j0 + P].bitcast(FP8X4), rhs_scale=vs[4 * a : P, j0 : j0 + P],
+                        nc.tensor.matmul_mx(out=bank[:, t, :], lhsT=codes[:, P * t : P * (t + 1)].bitcast(FP8X4), lhsT_scale=scales[:, P * t : P * (t + 1)],
+                                            rhs=v_words[a][:, j0 : j0 + P].bitcast(FP8X4), rhs_scale=v_scales[4 * a : P, j0 : j0 + P],
                                             start=(a == 0 and t == 0), stop=(a == 1 and t == 3))
-                lp = ring.tile([P, 4, P], F32, name="lp")
+                leaked = ring.tile([P, 4, P], F32, name="leaked", bufs=4)
                 for t in range(4):
-                    nc.scalar.activation(out=lp[:, t, :], in_=bank[:, t, :], func=ACT.Copy, scale=leak_t[:, b, t : t + 1])
-                nc.vector.tensor_tensor(out=hb[:, P * jq : P * jq + P, :].rearrange("p (c i) t -> p c t i", i=2),
-                                        in0=bank[:].rearrange("p t (c i) -> p c t i", i=2),
-                                        in1=lp[:].rearrange("p t (c i) -> p c t i", i=2), op=ALU.max)
-            return hb
+                    nc.scalar.activation(out=leaked[:, t, :], in_=bank[:, t, :], func=ACT.Copy, scale=leak_t[:, b, t : t + 1])
+                nc.vector.tensor_tensor(out=h_bf[:, P * jq : P * (jq + 1), :].rearrange("p (c e) t -> p c t e", e=2),
+                                        in0=bank[:].rearrange("p t (c e) -> p c t e", e=2),
+                                        in1=leaked[:].rearrange("p t (c e) -> p c t e", e=2), op=ALU.max)
+            return h_bf
 
-        def hquant(hb, b, jh):
-            hq[(b, jh)] = quant(hb[:].rearrange("p j t -> p (j t)"), 512, "hq%d%d" % (b, jh))
+        def quantise_h(h_bf, b, jh):
+            h_q[(b, jh)] = quantise(h_bf[:].rearrange("p j t -> p (j t)"), "h%d%d" % (b, jh))
 
-        e_t = [kt([P, S], F32, "e%d" % t) for t in range(4)]
-        d_t = [kt([P, S], F32, "d%d" % t) for t in range(4)]
-        wbq = {}
+        e_t = [kept([P, S], F32, "e%d" % t) for t in range(4)]
+        d_t = [kept([P, S], F32, "d%d" % t) for t in range(4)]
+        wb_q = {}
 
         def e_part(t, jh):
-            bank = ps2.tile([P, 512], F32, name="bank2")
+            bank = psum.tile([P, PASS], F32, name="bank_e", tag="bank")
             for b in range(2):
-                codes, scales = hq[(b, jh)]
-                nc.tensor.matmul_mx(out=bank[:], lhsT=waw[:, b, 256 * t : 256 * t + 256].bitcast(FP4X4), lhsT_scale=was[:, b, P * t : P * t + P],
+                codes, scales = h_q[(b, jh)]
+                nc.tensor.matmul_mx(out=bank[:], lhsT=wa_w[:, b, 2 * P * t : 2 * P * (t + 1)].bitcast(FP4X4), lhsT_scale=wa_s[:, b, P * t : P * (t + 1)],
                                     rhs=codes[:].bitcast(FP8X4), rhs_scale=scales[:], start=(b == 0), stop=(b == 1))
-            nc.scalar.copy(out=e_t[t][:, 512 * jh : 512 * jh + 512], in_=bank[:])
+            nc.scalar.copy(out=e_t[t][:, PASS * jh : PASS * (jh + 1)], in_=bank[:])
 
         def d_part(t, jh):
-            bank = ps2.tile([P, 512], F32, name="bank2")
+            bank = psum.tile([P, PASS], F32, name="bank_d", tag="bank")
             for b in range(2):
-                codes, scales = hq[(b, jh)]
-                wc, ws = wbq[b]
-                nc.tensor.matmul_mx(out=bank[:], lhsT=wc[:, P * t : P * t + P].bitcast(FP8X4), lhsT_scale=ws[:, P * t : P * t + P],
+                codes, scales = h_q[(b, jh)]
+                wb_codes, wb_scales = wb_q[b]
+                nc.tensor.matmul_mx(out=bank[:], lhsT=wb_codes[:, P * t : P * (t + 1)].bitcast(FP8X4), lhsT_scale=wb_scales[:, P * t : P * (t + 1)],
                                     rhs=codes[:].bitcast(FP8X4), rhs_scale=scales[:], start=(b == 0), stop=(b == 1))
-            cols = slice(512 * jh, 512 * jh + 512)
+            cols = slice(PASS * jh, PASS * (jh + 1))
             nc.vector.tensor_tensor(out=d_t[t][:, cols], in0=bank[:], in1=site_t[t][:, cols], op=ALU.add)
 
-        def quarters(name, raw, engines):
-            return weight(name, [(engines[i], raw, 256 * (i % 2), i // 2, 64 * (i % 2), 64 * (i % 2) + 64) for i in range(4)])
-
-        hb00 = stage1(0, 0)
-        g01 = quarters("w01", w1_raw[(0, 1, 0)], "ssvv")
-        hquant(hb00, 0, 0)
-        w1q[(0, 1)] = wq(g01, "w01")
-        g11 = quarters("w11", w1_raw[(1, 1, 0)], "ssvv")
-        hb01 = stage1(0, 1)
-        w1q[(1, 1)] = wq(g11, "w11")
-        hb10 = stage1(1, 0)
-        hquant(hb01, 0, 1)
-        gb0 = quarters("wb0", wb_raw[0], "sssv")
-        hquant(hb10, 1, 0)
-        gb1 = quarters("wb1", wb_raw[1], "sssv")
-        hb11 = stage1(1, 1)
-        wbq[0] = wq(gb0, "wb0")
-        wbq[1] = wq(gb1, "wb1")
-        hquant(hb11, 1, 1)
-        nc.vector.tensor_copy(out=was[:].rearrange("p a (t m) -> p a t m", t=4), in_=was_raw[:].rearrange("p a (m t) -> p a t m", t=4))
+        h00 = first_stage(0, 0)
+        w1_01 = cast_quarters("w1_01", w1_raw[(0, 1, 0)], W1_LATE_SHARE)
+        quantise_h(h00, 0, 0)
+        w1_q[(0, 1)] = quantise_weight(w1_01, "w1_01")
+        w1_11 = cast_quarters("w1_11", w1_raw[(1, 1, 0)], W1_LATE_SHARE)
+        h01 = first_stage(0, 1)
+        w1_q[(1, 1)] = quantise_weight(w1_11, "w1_11")
+        h10 = first_stage(1, 0)
+        quantise_h(h01, 0, 1)
+        wb_0 = cast_quarters("wb_0", wb_raw[0], WB_SHARE)
+        quantise_h(h10, 1, 0)
+        wb_1 = cast_quarters("wb_1", wb_raw[1], WB_SHARE)
+        h11 = first_stage(1, 1)
+        wb_q[0] = quantise_weight(wb_0, "wb_0")
+        wb_q[1] = quantise_weight(wb_1, "wb_1")
+        quantise_h(h11, 1, 1)
         for t in range(4):
             d_part(t, 0)
             e_part(t, 0)
 
-        y = kt([P, 4, NP], F32, "y", "tabw0")
-        out_v = out_0.rearrange("(p t) m -> t p m", t=4)
-        yb = kt([P, NP, 4], BF16, "yb", "tabw1")
-        ycodes = kt([P, NP], U32, "ycodes")
-        yscales = kt([P, NP], U8, "yscales")
-        words_v = out_1[0].rearrange("p m t -> p (m t)").bitcast(I32)
-
+        y = kept([P, 4, NP], F32, "y", "table_words0")
+        out_rows = out_0.rearrange("(p t) m -> t p m", t=4)
+        y_bf = kept([P, NP, 4], BF16, "y_bf", "table_words1")
+        y_codes = kept([P, NP], U32, "y_codes")
+        y_scales = kept([P, NP], U8, "y_scales")
+        words_out = out_1[0].rearrange("p m t -> p (m t)").bitcast(I32)
         picked = {}
 
         def pick(t, m0, m1):
-            w = m1 - m0
-            c = ring.tile([P, w], F32, name="c")
-            gate = ring.tile([P, w], F32, name="gate")
-            lc = slice(m0 // 16, m1 // 16)
-            nc.vector.tensor_copy(out=c[:], in_=d_t[t][:].indirect(pos2_t[:, lc]))
-            nc.scalar.activation(out=gate[:], in_=e_t[t][:].indirect(pos1_t[:, lc]), func=ACT.Sigmoid, bias=thresh_t[:, t : t + 1], scale=steep_t[:, t : t + 1])
-            picked[(t, m0)] = [c, gate]
+            corridor = ring.tile([P, m1 - m0], F32, name="corridor")
+            gate = ring.tile([P, m1 - m0], F32, name="gate")
+            entries = slice(m0 // LIST, m1 // LIST)
+            nc.vector.tensor_copy(out=corridor[:], in_=d_t[t][:].indirect(pos2_t[:, entries]))
+            nc.scalar.activation(out=gate[:], in_=e_t[t][:].indirect(pos1_t[:, entries]), func=ACT.Sigmoid,
+                                 bias=thresh_t[:, t : t + 1], scale=steep_t[:, t : t + 1])
+            picked[(t, m0)] = [corridor, gate]
 
         def cap(t, m0, m1):
-            c, gate = picked[(t, m0)]
-            z = ring.tile([P, m1 - m0], F32, name="z")
-            nc.vector.scalar_tensor_tensor(out=z[:], in0=gate[:], scalar=swing_t[:, t : t + 1], in1=c[:], op0=ALU.mult, op1=ALU.min)
-            picked[(t, m0)].append(z)
+            corridor, gate = picked[(t, m0)]
+            capped = ring.tile([P, m1 - m0], F32, name="capped")
+            nc.vector.scalar_tensor_tensor(out=capped[:], in0=gate[:], scalar=swing_t[:, t : t + 1], in1=corridor[:], op0=ALU.mult, op1=ALU.min)
+            picked[(t, m0)] = [corridor, capped]
 
         def total(t, m0, m1):
-            c, gate, z = picked[(t, m0)]
-            nc.vector.tensor_tensor(out=y[:, t, m0:m1], in0=z[:], in1=c[:], op=ALU.add)
-            nc.sync.dma_start(out=out_v[t][:, m0:m1], in_=y[:, t, m0:m1])
+            corridor, capped = picked[(t, m0)]
+            nc.vector.tensor_tensor(out=y[:, t, m0:m1], in0=capped[:], in1=corridor[:], op=ALU.add)
+            nc.sync.dma_start(out=out_rows[t][:, m0:m1], in_=y[:, t, m0:m1])
 
-        def planes(m0, m1, on_scalar):
-            o = yb[:, m0:m1, :].rearrange("p (c i) t -> p c t i", i=2)
-            i_ = y[:, :, m0:m1].rearrange("p t (c i) -> p c t i", i=2)
-            if on_scalar:
-                nc.scalar.copy(out=o, in_=i_)
-            else:
-                nc.vector.tensor_copy(out=o, in_=i_)
+        def round_views(m0, m1):
+            return (y_bf[:, m0:m1, :].rearrange("p (c e) t -> p c t e", e=2), y[:, :, m0:m1].rearrange("p t (c e) -> p c t e", e=2))
 
-        def pquant(m0, m1):
-            nc.vector.quantize_mx(out=ycodes[:, m0:m1].bitcast(FP8X4), scales=yscales[:, m0:m1], in_=yb[:, m0:m1, :].rearrange("p m t -> p (m t)"))
-            nc.sync.dma_start(out=words_v[:, m0:m1], in_=ycodes[:, m0:m1].bitcast(I32))
-
-        units = [(0, 0, 512), (1, 0, 512), (2, 0, 512), (3, 0, 256), (3, 256, 512)]
-        for step in range(len(units) + 3):
+        y_blocks = [(t, 0, NP) for t in range(3)] + [(3, 0, HALF_NP), (3, HALF_NP, NP)]
+        for step in range(len(y_blocks) + 3):
             if step < 4:
                 e_part(step, 1)
                 d_part(step, 1)
-            if 3 <= step:
-                total(*units[step - 3])
-            if 1 <= step <= len(units):
-                pick(*units[step - 1])
-            if 2 <= step <= len(units) + 1:
-                cap(*units[step - 2])
-            if step == len(units) + 1:
-                planes(0, 256, True)
-        planes(256, 512, False)
-        pquant(0, 256)
-        pquant(256, 512)
-        for q in range(4):
-            eng = nc.scalar if q % 2 else nc.sync
-            eng.dma_start(out=out_2[0, 4 * q : 4 * q + 4, :].bitcast(I32), in_=yscales[32 * q : 32 * q + 4, :].bitcast(I32))
+            if step >= 3:
+                total(*y_blocks[step - 3])
+            if 1 <= step <= len(y_blocks):
+                pick(*y_blocks[step - 1])
+            if 2 <= step <= len(y_blocks) + 1:
+                cap(*y_blocks[step - 2])
+            if step == len(y_blocks) + 1:
+                dst, src = round_views(0, HALF_NP)
+                nc.scalar.copy(out=dst, in_=src)
+        dst, src = round_views(HALF_NP, NP)
+        nc.vector.tensor_copy(out=dst, in_=src)
+        for m0 in (0, HALF_NP):
+            cols = slice(m0, m0 + HALF_NP)
+            nc.vector.quantize_mx(out=y_codes[:, cols].bitcast(FP8X4), scales=y_scales[:, cols], in_=y_bf[:, cols, :].rearrange("p m t -> p (m t)"))
+            nc.sync.dma_start(out=words_out[:, cols], in_=y_codes[:, cols].bitcast(I32))
+        for quadrant in range(4):
+            queue = nc.scalar if quadrant % 2 else nc.sync
+            queue.dma_start(out=out_2[0, 4 * quadrant : 4 * quadrant + 4, :].bitcast(I32), in_=y_scales[32 * quadrant : 32 * quadrant + 4, :].bitcast(I32))

from contextlib import ExitStack

import concourse.mybir as mybir

F32 = mybir.dt.float32
BF16 = mybir.dt.bfloat16
I32 = mybir.dt.int32
U32 = mybir.dt.uint32
U16 = mybir.dt.uint16
U8 = mybir.dt.uint8
FP8X4 = mybir.dt.float8_e4m3fn_x4
FP4X4 = mybir.dt.float4_e2m1fn_x4
ALU = mybir.AluOpType
ACT = mybir.ActivationFunctionType

K, T, S, NP, H, N = 1024, 4096, 1024, 512, 1024, 512
FLOPS = 2 * K * H * S + 2 * 2 * H * N * S
P = 128
PASS = 512
HALF_M = P // 2
HALF_NP = NP // 2
LIST = 16

W1_LATE_SHARE = "ssvv"
WB_SHARE = "sssv"


def cast_piece(nc, engine, dealt, raw, pair, m0, m1):
    dst = dealt[:, 2 * pair : 2 * pair + 2, m0:m1, :].rearrange("p t m i -> p m i t")
    src = raw.rearrange("p i (m t) -> p m i t", t=4)[:, :, :, 2 * pair : 2 * pair + 2]
    if engine == "v":
        nc.vector.tensor_copy(out=dst, in_=src)
    else:
        nc.scalar.copy(out=dst, in_=src)


def tile_list_roaming_gate_scores_kernel(tc, tab_words, tab_scales, offs, pos1, pos2, w1, leak, wa_words, wa_scales, wb, site, steep, thresh, swing, out_0, out_1, out_2):
    nc = tc.nc
    with ExitStack() as ctx:
        keep = ctx.enter_context(tc.tile_pool(name="keep", bufs=1))
        ring = ctx.enter_context(tc.tile_pool(name="ring", bufs=3))
        psum = ctx.enter_context(tc.psum_pool(name="psum", bufs=8))

        def kept(shape, dtype, name, tag=None):
            return keep.tile(shape, dtype, name=name, tag=tag or name, align_bytes=64)

        offs_t = keep.tile([P, S // LIST], U16, name="offs_t")
        pos1_t = keep.tile([P, NP // LIST], U16, name="pos1_t")
        pos2_t = keep.tile([P, NP // LIST], U16, name="pos2_t")
        table_words = [kept([P, T], I32, "table_words%d" % a) for a in range(2)]
        table_scales = kept([P, T], U8, "table_scales")
        wa_scales_raw = kept([P, 2, N], U8, "wa_scales_raw")
        wa_words_raw = kept([P, 2, 2 * N], U8, "wa_words_raw")
        nc.vector.memset(table_scales[:].bitcast(I32), 0)
        nc.vector.memset(wa_scales_raw[:].bitcast(I32), 0)

        w1_raw = {}

        def load_w1(a, b, part, parts):
            width = PASS // parts
            raw = kept([P, 4, width], F32, "w1_raw%d%d%d" % (a, b, part))
            c0 = PASS * b + width * part
            nc.sync.dma_start(out=raw[:], in_=w1[PASS * a : PASS * (a + 1), c0 : c0 + width].rearrange("(p i) c -> p i c", i=4))
            w1_raw[(a, b, part)] = raw

        def load_rows(values, name):
            dealt = kept([P, 4], F32, name)
            nc.sync.dma_start(out=dealt[:], in_=values.rearrange("(p t) -> p t", t=4))
            return dealt

        scale_stage = kept([P, T // 4], I32, "scale_stage")

        def load_scale_rows(quadrant):
            for a in range(2):
                row = 32 * quadrant + 4 * a
                nc.sync.dma_start(out=scale_stage[row : row + 4, :], in_=tab_scales[a, 4 * quadrant : 4 * quadrant + 4, :].bitcast(I32))

        words_in = [tab_words[a].rearrange("p c i -> p (c i)").bitcast(I32) for a in range(2)]
        nc.sync.dma_start(offs_t[:], offs)
        for quadrant in range(3):
            load_scale_rows(quadrant)
        nc.sync.dma_start(out=table_words[0][:, : T // 2], in_=words_in[0][:, : T // 2])
        load_scale_rows(3)
        nc.sync.dma_start(out=table_words[0][:, T // 2 :], in_=words_in[0][:, T // 2 :])
        nc.sync.dma_start(out=wa_words_raw[:].bitcast(I32), in_=wa_words.rearrange("a p c -> p a c").bitcast(I32))
        for quadrant in range(4):
            nc.sync.dma_start(out=wa_scales_raw[32 * quadrant : 32 * quadrant + 4].bitcast(I32),
                              in_=wa_scales[:, 4 * quadrant : 4 * quadrant + 4, :].rearrange("a r c -> r a c").bitcast(I32))
        nc.sync.dma_start(out=table_words[1][:], in_=words_in[1])
        load_w1(0, 0, 0, 1)
        load_w1(1, 0, 0, 2)
        load_w1(1, 0, 1, 2)
        leak_t = kept([P, 2, 4], F32, "leak_t")
        nc.sync.dma_start(out=leak_t[:], in_=leak.rearrange("(b p t) -> p b t", b=2, t=4))
        load_w1(0, 1, 0, 1)
        load_w1(1, 1, 0, 1)
        wb_raw = []
        for b in range(2):
            raw = kept([P, 4, N], F32, "wb_raw%d" % b)
            nc.sync.dma_start(out=raw[:], in_=wb[PASS * b : PASS * (b + 1), :].rearrange("(p i) c -> p i c", i=4))
            wb_raw.append(raw)
        nc.sync.dma_start(pos1_t[:], pos1)
        nc.sync.dma_start(pos2_t[:], pos2)
        steep_t = load_rows(steep, "steep_t")
        thresh_t = load_rows(thresh, "thresh_t")
        swing_t = load_rows(swing, "swing_t")
        site_rows = site.rearrange("(p t) j -> t p j", t=4)
        site_t = []
        for t, spent in enumerate(("w1_raw000", "w1_raw100", "w1_raw101", "scale_stage")):
            rows = kept([P, S], F32, "site%d" % t, spent)
            nc.sync.dma_start(out=rows[:], in_=site_rows[t])
            site_t.append(rows)

        for quadrant in range(4):
            live = slice(32 * quadrant, 32 * quadrant + 8)
            nc.vector.tensor_copy(out=table_scales[live, :].bitcast(I32), in_=scale_stage[live, :])
        wa_w = kept([P, 2, 2 * N], U8, "wa_w")
        v_scales = kept([P, S], U8, "v_scales")
        nc.vector.tensor_copy(out=v_scales[:], in_=table_scales[:].indirect(offs_t[:]))
        nc.vector.tensor_copy(out=wa_w[:].rearrange("p a c -> p (a c)").bitcast(U16).rearrange("p (a t m) -> p a t m", a=2, t=4),
                              in_=wa_words_raw[:].rearrange("p a c -> p (a c)").bitcast(U16).rearrange("p (a m t) -> p a t m", a=2, t=4))
        v_words = [kept([P, S], U32, "v_words%d" % a) for a in range(2)]
        nc.vector.tensor_copy(out=v_words[0][:], in_=table_words[0][:].bitcast(U32).indirect(offs_t[:]))
        wa_s = kept([P, 2, N], U8, "wa_s")
        nc.vector.tensor_copy(out=wa_s[:].rearrange("p a (t m) -> p a t m", t=4), in_=wa_scales_raw[:].rearrange("p a (m t) -> p a t m", t=4))
        nc.vector.tensor_copy(out=v_words[1][:], in_=table_words[1][:].bitcast(U32).indirect(offs_t[:]))

        def quantise(values, name, parts=1):
            codes = kept([P, PASS], U32, name + "_codes")
            scales = kept([P, PASS], U8, name + "_scales")
            width = PASS // parts
            for part in range(parts):
                cols = slice(width * part, width * (part + 1))
                nc.vector.quantize_mx(out=codes[:, cols].bitcast(FP8X4), scales=scales[:, cols], in_=values[:, 4 * cols.start : 4 * cols.stop])
            return codes, scales

        def cast_weight(name, pieces):
            dealt = kept([P, 4, P, 4], BF16, name + "_dealt")
            for engine, raw, c0, pair, m0, m1 in pieces:
                cast_piece(nc, engine, dealt, raw[:, :, c0 : c0 + 4 * (m1 - m0)], pair, m0, m1)
            return dealt

        def cast_quarters(name, raw, share):
            return cast_weight(name, [(share[2 * pair + half], raw, 4 * HALF_M * half, pair, HALF_M * half, HALF_M * (half + 1))
                                      for pair in range(2) for half in range(2)])

        def quantise_weight(dealt, name, parts=1):
            return quantise(dealt[:].rearrange("p t m i -> p (t m i)"), name, parts)

        w1_q = {}
        raw = w1_raw[(0, 0, 0)]
        w1_q[(0, 0)] = quantise_weight(cast_weight("w1_00", [("s", raw, 0, 0, 0, P), ("v", raw, 0, 1, 0, P)]), "w1_00")
        pieces = [(engine, w1_raw[(1, 0, half)], 0, pair, HALF_M * half, HALF_M * (half + 1)) for half in range(2) for pair, engine in enumerate("vs")]
        w1_q[(1, 0)] = quantise_weight(cast_weight("w1_10", pieces), "w1_10", 2)

        h_q = {}

        def first_stage(b, jh):
            h_bf = kept([P, PASS, 4], BF16, "h_bf%d%d" % (b, jh))
            for jq in range(4):
                j0 = PASS * jh + P * jq
                bank = psum.tile([P, 4, P], F32, name="bank_h", tag="bank")
                for a in range(2):
                    codes, scales = w1_q[(a, b)]
                    for t in range(4):
                        nc.tensor.matmul_mx(out=bank[:, t, :], lhsT=codes[:, P * t : P * (t + 1)].bitcast(FP8X4), lhsT_scale=scales[:, P * t : P * (t + 1)],
                                            rhs=v_words[a][:, j0 : j0 + P].bitcast(FP8X4), rhs_scale=v_scales[4 * a : P, j0 : j0 + P],
                                            start=(a == 0 and t == 0), stop=(a == 1 and t == 3))
                leaked = ring.tile([P, 4, P], F32, name="leaked", bufs=4)
                for t in range(4):
                    nc.scalar.activation(out=leaked[:, t, :], in_=bank[:, t, :], func=ACT.Copy, scale=leak_t[:, b, t : t + 1])
                nc.vector.tensor_tensor(out=h_bf[:, P * jq : P * (jq + 1), :].rearrange("p (c e) t -> p c t e", e=2),
                                        in0=bank[:].rearrange("p t (c e) -> p c t e", e=2),
                                        in1=leaked[:].rearrange("p t (c e) -> p c t e", e=2), op=ALU.max)
            return h_bf

        def quantise_h(h_bf, b, jh):
            h_q[(b, jh)] = quantise(h_bf[:].rearrange("p j t -> p (j t)"), "h%d%d" % (b, jh))

        e_t = [kept([P, S], F32, "e%d" % t) for t in range(4)]
        d_t = [kept([P, S], F32, "d%d" % t) for t in range(4)]
        wb_q = {}

        def e_part(t, jh):
            bank = psum.tile([P, PASS], F32, name="bank_e", tag="bank")
            for b in range(2):
                codes, scales = h_q[(b, jh)]
                nc.tensor.matmul_mx(out=bank[:], lhsT=wa_w[:, b, 2 * P * t : 2 * P * (t + 1)].bitcast(FP4X4), lhsT_scale=wa_s[:, b, P * t : P * (t + 1)],
                                    rhs=codes[:].bitcast(FP8X4), rhs_scale=scales[:], start=(b == 0), stop=(b == 1))
            nc.scalar.copy(out=e_t[t][:, PASS * jh : PASS * (jh + 1)], in_=bank[:])

        def d_part(t, jh):
            bank = psum.tile([P, PASS], F32, name="bank_d", tag="bank")
            for b in range(2):
                codes, scales = h_q[(b, jh)]
                wb_codes, wb_scales = wb_q[b]
                nc.tensor.matmul_mx(out=bank[:], lhsT=wb_codes[:, P * t : P * (t + 1)].bitcast(FP8X4), lhsT_scale=wb_scales[:, P * t : P * (t + 1)],
                                    rhs=codes[:].bitcast(FP8X4), rhs_scale=scales[:], start=(b == 0), stop=(b == 1))
            cols = slice(PASS * jh, PASS * (jh + 1))
            nc.vector.tensor_tensor(out=d_t[t][:, cols], in0=bank[:], in1=site_t[t][:, cols], op=ALU.add)

        h00 = first_stage(0, 0)
        w1_01 = cast_quarters("w1_01", w1_raw[(0, 1, 0)], W1_LATE_SHARE)
        quantise_h(h00, 0, 0)
        w1_q[(0, 1)] = quantise_weight(w1_01, "w1_01")
        w1_11 = cast_quarters("w1_11", w1_raw[(1, 1, 0)], W1_LATE_SHARE)
        h01 = first_stage(0, 1)
        w1_q[(1, 1)] = quantise_weight(w1_11, "w1_11")
        h10 = first_stage(1, 0)
        quantise_h(h01, 0, 1)
        wb_0 = cast_quarters("wb_0", wb_raw[0], WB_SHARE)
        quantise_h(h10, 1, 0)
        wb_1 = cast_quarters("wb_1", wb_raw[1], WB_SHARE)
        h11 = first_stage(1, 1)
        wb_q[0] = quantise_weight(wb_0, "wb_0")
        wb_q[1] = quantise_weight(wb_1, "wb_1")
        quantise_h(h11, 1, 1)
        for t in range(4):
            d_part(t, 0)
            e_part(t, 0)

        y = kept([P, 4, NP], F32, "y", "table_words0")
        out_rows = out_0.rearrange("(p t) m -> t p m", t=4)
        y_bf = kept([P, NP, 4], BF16, "y_bf", "table_words1")
        y_codes = kept([P, NP], U32, "y_codes")
        y_scales = kept([P, NP], U8, "y_scales")
        words_out = out_1[0].rearrange("p m t -> p (m t)").bitcast(I32)
        picked = {}

        def pick(t, m0, m1):
            corridor = ring.tile([P, m1 - m0], F32, name="corridor")
            gate = ring.tile([P, m1 - m0], F32, name="gate")
            entries = slice(m0 // LIST, m1 // LIST)
            nc.vector.tensor_copy(out=corridor[:], in_=d_t[t][:].indirect(pos2_t[:, entries]))
            nc.scalar.activation(out=gate[:], in_=e_t[t][:].indirect(pos1_t[:, entries]), func=ACT.Sigmoid,
                                 bias=thresh_t[:, t : t + 1], scale=steep_t[:, t : t + 1])
            picked[(t, m0)] = [corridor, gate]

        def cap(t, m0, m1):
            corridor, gate = picked[(t, m0)]
            capped = ring.tile([P, m1 - m0], F32, name="capped")
            nc.vector.scalar_tensor_tensor(out=capped[:], in0=gate[:], scalar=swing_t[:, t : t + 1], in1=corridor[:], op0=ALU.mult, op1=ALU.min)
            picked[(t, m0)] = [corridor, capped]

        def total(t, m0, m1):
            corridor, capped = picked[(t, m0)]
            nc.vector.tensor_tensor(out=y[:, t, m0:m1], in0=capped[:], in1=corridor[:], op=ALU.add)
            nc.sync.dma_start(out=out_rows[t][:, m0:m1], in_=y[:, t, m0:m1])

        def round_views(m0, m1):
            return (y_bf[:, m0:m1, :].rearrange("p (c e) t -> p c t e", e=2), y[:, :, m0:m1].rearrange("p t (c e) -> p c t e", e=2))

        y_blocks = [(t, 0, NP) for t in range(3)] + [(3, 0, HALF_NP), (3, HALF_NP, NP)]
        for step in range(len(y_blocks) + 3):
            if step < 4:
                e_part(step, 1)
                d_part(step, 1)
            if step >= 3:
                total(*y_blocks[step - 3])
            if 1 <= step <= len(y_blocks):
                pick(*y_blocks[step - 1])
            if 2 <= step <= len(y_blocks) + 1:
                cap(*y_blocks[step - 2])
            if step == len(y_blocks) + 1:
                dst, src = round_views(0, HALF_NP)
                nc.scalar.copy(out=dst, in_=src)
        dst, src = round_views(HALF_NP, NP)
        nc.vector.tensor_copy(out=dst, in_=src)
        for m0 in (0, HALF_NP):
            cols = slice(m0, m0 + HALF_NP)
            nc.vector.quantize_mx(out=y_codes[:, cols].bitcast(FP8X4), scales=y_scales[:, cols], in_=y_bf[:, cols, :].rearrange("p m t -> p (m t)"))
            nc.sync.dma_start(out=words_out[:, cols], in_=y_codes[:, cols].bitcast(I32))
        for quadrant in range(4):
            queue = nc.scalar if quadrant % 2 else nc.sync
            queue.dma_start(out=out_2[0, 4 * quadrant : 4 * quadrant + 4, :].bitcast(I32), in_=y_scales[32 * quadrant : 32 * quadrant + 4, :].bitcast(I32))
